import numpy as np
import ml_dtypes


def mxq(x, axis, fmt="e4m3"):
    dtype, down = {"e4m3": (ml_dtypes.float8_e4m3fn, 7), "e5m2": (ml_dtypes.float8_e5m2, 14)}[fmt]
    v = np.moveaxis(np.asarray(x, np.float32).astype(ml_dtypes.bfloat16).astype(np.float64), axis, -1)
    blocks = v.reshape(v.shape[:-1] + (-1, 32))
    amax = np.abs(blocks).max(-1, keepdims=True)
    byte = np.maximum(np.where(amax > 0, np.frexp(amax)[1] - 1 + 127, 0) - down, 1)
    scale = np.exp2(byte - 127.0)
    codes = (blocks / scale).astype(np.float32).astype(dtype).astype(np.float64)
    return np.moveaxis((codes * scale).reshape(v.shape), -1, axis)


WIDE = False


def mx_kscale(k):
    if not WIDE:
        return np.ones(k)
    levels = np.array([10, -10, 5, -5, 0])
    if k % 512:
        return np.exp2(np.random.permutation(np.resize(levels, k // 32))).repeat(32)
    a = np.empty((k // 512, 16))
    for p in range(k // 512):
        a[p, :8] = np.random.permutation(np.resize(levels, 8))
        for g in range(8):
            far = levels[np.abs(levels - a[p, g]) >= 10]
            a[p, g + 8] = far[np.random.randint(len(far))]
    return np.exp2(a.ravel()).repeat(32)


def f64(x):
    return np.asarray(x).astype(np.float64)


def striped(idx):
    return np.tile(np.asarray(idx).reshape(-1, 16).T, (8, 1)).astype(np.uint16)


def unstriped(offs):
    return offs[:16].T.reshape(-1).astype(np.int64)


E2M1 = np.array([0.0, 0.5, 1.0, 1.5, 2.0, 3.0, 4.0, 6.0, -0.0, -0.5, -1.0, -1.5, -2.0, -3.0, -4.0, -6.0])


def pack_weight(w, fmt):
    k, n = w.shape
    w = f64(np.asarray(w, np.float32).astype(ml_dtypes.bfloat16)).reshape(k // 32, 32, n)
    amax = np.abs(w).max(1)
    if fmt == "e4m3":
        byte = np.frexp(amax)[1] - 1 + 127 - 7
    else:
        mant, ex = np.frexp(amax / 6.0)
        byte = np.where(mant > 0.5, ex, ex - 1) + 127
    byte = np.clip(np.where(amax > 0, byte, 1), 1, 254)
    scaled = (w * np.exp2(127.0 - byte)[:, None, :]).reshape(k, n).astype(np.float32)
    by_word = np.ascontiguousarray(scaled.reshape(k // 512, 128, 4, n).transpose(0, 1, 3, 2))
    if fmt == "e4m3":
        words = by_word.astype(ml_dtypes.float8_e4m3fn).view(np.uint8)
    else:
        c = by_word.astype(ml_dtypes.float4_e2m1fn).view(np.uint8) & 0xF
        words = (c[..., 0::2] | (c[..., 1::2] << 4)).reshape(k // 512, 128, 2 * n)
    return np.ascontiguousarray(words), np.ascontiguousarray(byte.astype(np.uint8).reshape(k // 512, 16, n))


def unpack_weight(words, scales, fmt):
    g, _, n = scales.shape
    words = np.ascontiguousarray(words).reshape(g, 128, n, -1)
    if fmt == "e4m3":
        vals = words.view(ml_dtypes.float8_e4m3fn).astype(np.float64)
    else:
        nib = np.empty((g, 128, n, 4), np.uint8)
        nib[..., 0::2] = words & 0xF
        nib[..., 1::2] = words >> 4
        vals = E2M1[nib]
    vals = vals * np.repeat(np.exp2(scales.astype(np.float64) - 127.0), 8, axis=1)[..., None]
    return vals.transpose(0, 1, 3, 2).reshape(g * 512, n)


K, T, J, N, R = 1024, 2048, 512, 512, 512


def setup_inputs():
    n = np.random.standard_normal
    idx = np.random.permutation(T)[:J]
    fk = mx_kscale(K)
    fr = mx_kscale(R)
    xqp = pack_weight(n((K, T)) / fk[:, None], "e4m3")
    wap = pack_weight(n((K, R)) * 1 / np.sqrt(K) * fk[:, None] * fr, "e2m1")
    wbp = pack_weight(n((R, N)) * 1 / np.sqrt(R) / fr[:, None], "e4m3")
    wcp = pack_weight(n((K, N)) * 1 / np.sqrt(K) * fk[:, None], "e2m1")
    return {
        "xq_words": xqp[0],
        "xq_scales": xqp[1],
        "wa_words": wap[0],
        "wa_scales": wap[1],
        "wb_words": wbp[0],
        "wb_scales": wbp[1],
        "wc_words": wcp[0],
        "wc_scales": wcp[1],
        "ga": (np.random.uniform(0.4, 1.2, (1, J))).astype(np.float32),
        "offs": striped(idx),
    }


def reference(xq_words, xq_scales, wa_words, wa_scales, wb_words, wb_scales, wc_words, wc_scales, ga, offs):
    idx = unstriped(offs)
    xqu = unpack_weight(xq_words, xq_scales, "e4m3")
    wau = unpack_weight(wa_words, wa_scales, "e2m1")
    wbu = unpack_weight(wb_words, wb_scales, "e4m3")
    wcu = unpack_weight(wc_words, wc_scales, "e2m1")
    xqidxg = xqu[:, idx]
    a = wau.T @ xqidxg
    hid = np.maximum(a, 0.0)
    hidq = mxq(hid, 0, "e4m3")
    p = wbu.T @ hidq + wcu.T @ xqidxg
    y = p * f64(ga)
    return y

@@ -1,0 +1,192 @@
+from contextlib import ExitStack
+
+import concourse.mybir as mybir
+from concourse.masks import make_identity
+
+K, T, J, N, R = 1024, 2048, 512, 512, 512
+FLOPS = 2 * J * (K * R + R * N + K * N)
+
+F32 = mybir.dt.float32
+BF16 = mybir.dt.bfloat16
+I32 = mybir.dt.int32
+U32 = mybir.dt.uint32
+U16 = mybir.dt.uint16
+U8 = mybir.dt.uint8
+FP8X4 = mybir.dt.float8_e4m3fn_x4
+FP4X4 = mybir.dt.float4_e2m1fn_x4
+
+P = 128
+PACK = 4
+PASSES = K // (P * PACK)
+QUADRANTS = 4
+BLOCK = 128
+BLOCKS = J // BLOCK
+HALF = 256
+N_TILES = N // P
+
+
+def tile_list_expert_with_bypass_kernel(
+    tc, xq_words, xq_scales, wa_words, wa_scales, wb_words, wb_scales, wc_words, wc_scales, ga, offs, out
+):
+    nc = tc.nc
+    with ExitStack() as ctx:
+        keep = ctx.enter_context(tc.tile_pool(name="keep", bufs=1))
+        psum = ctx.enter_context(tc.psum_pool(name="psum", bufs=1))
+
+        def sbuf(name, shape, dtype):
+            return keep.tile(shape, dtype, name=name, align_bytes=64)
+
+        offsets = keep.tile([P, J // 16], U16, name="offsets")
+        x_table = [sbuf("x_table%d" % z, [P, T], I32) for z in range(PASSES)]
+        x_table_scales = sbuf("x_table_scales", [P, T], U8)
+        wa_raw = sbuf("wa_raw", [P, PASSES, 2 * R], U8)
+        wa_raw_scales = sbuf("wa_raw_scales", [P, PASSES, R], U8)
+        wc_codes = [sbuf("wc_codes%d" % z, [P, 2 * N], U8) for z in range(PASSES)]
+        wc_plane = sbuf("wc_plane", [P, PASSES, N], U8)
+        wb_codes = sbuf("wb_codes", [P, N], I32)
+        wb_plane = sbuf("wb_plane", [P, N], U8)
+        x_plane1 = sbuf("x_plane1", [P, J], U8)
+        ga_cols = sbuf("ga_cols", [P, PACK], F32)
+        identity = sbuf("identity", [P, P], F32)
+
+        a_banks = [psum.tile([P, PACK, BLOCK], F32, name="a_bank%d" % b) for b in range(BLOCKS)]
+        p_banks = [psum.tile([P, N_TILES, BLOCK], F32, name="p_bank%d" % b) for b in range(BLOCKS)]
+
+        for plane in (x_table_scales, wa_raw_scales, wc_plane, wb_plane, x_plane1):
+            nc.vector.memset(plane[:].bitcast(I32), 0)
+
+        def words(dram):
+            return dram.rearrange("p c t -> p (c t)").bitcast(I32)
+
+        def load_plane(queue, plane, scales):
+            for q in range(QUADRANTS):
+                queue.dma_start(
+                    out=plane[32 * q : 32 * q + 4].bitcast(I32),
+                    in_=scales[:, 4 * q : 4 * q + 4, :].rearrange("z r c -> r z c").bitcast(I32),
+                )
+
+        nc.sync.dma_start(out=wa_raw[:].bitcast(I32), in_=wa_words.rearrange("z p c -> p z c").bitcast(I32))
+        for q in range(QUADRANTS):
+            nc.scalar.dma_start(
+                out=x_table_scales[32 * q : 32 * q + 8, :].bitcast(I32),
+                in_=xq_scales[:, 4 * q : 4 * q + 4, :].bitcast(I32),
+            )
+        nc.sync.dma_start(offsets[:], offs)
+        nc.sync.dma_start(out=ga_cols[:], in_=ga[0].rearrange("(p c) -> p c", c=PACK))
+        nc.sync.dma_start(out=x_table[0][:], in_=words(xq_words[0]))
+        nc.sync.dma_start(out=wc_codes[0][:].bitcast(I32), in_=wc_words[0].bitcast(I32))
+        nc.sync.dma_start(out=x_table[1][:], in_=words(xq_words[1]))
+        load_plane(nc.scalar, wa_raw_scales, wa_scales)
+        make_identity(nc, identity[:])
+        load_plane(nc.gpsimd, wc_plane, wc_scales)
+        nc.sync.dma_start(out=wc_codes[1][:].bitcast(I32), in_=wc_words[1].bitcast(I32))
+        nc.sync.dma_start(out=wb_codes[:], in_=words(wb_words[0]))
+
+        x_plane0 = sbuf("x_plane0", [P, J], U8)
+        nc.vector.tensor_copy(out=x_plane0[:], in_=x_table_scales[:].indirect(offsets[:]))
+        nc.scalar.dma_start(out=x_plane1[0:100, :].bitcast(I32), in_=x_plane0[4:104, :].bitcast(I32))
+        x_planes = [x_plane0, x_plane1]
+        for q in range(QUADRANTS):
+            nc.scalar.dma_start(
+                out=wb_plane[32 * q : 32 * q + 4, :].bitcast(I32),
+                in_=wb_scales[0, 4 * q : 4 * q + 4, :].bitcast(I32),
+            )
+
+        x_codes = [[sbuf("x_codes%d_%d" % (z, h), [P, HALF], U32) for h in range(J // HALF)] for z in range(PASSES)]
+
+        def gather_words(z):
+            for h in range(J // HALF):
+                cols = slice(h * HALF // 16, (h + 1) * HALF // 16)
+                nc.vector.tensor_copy(out=x_codes[z][h][:], in_=x_table[z][:].bitcast(U32).indirect(offsets[:, cols]))
+
+        def x_operand(z, b):
+            h, i = divmod(b * BLOCK, HALF)
+            return x_codes[z][h][:, i : i + BLOCK].bitcast(FP8X4), x_planes[z][:, b * BLOCK : (b + 1) * BLOCK]
+
+        gather_words(0)
+
+        wa_codes = [sbuf("wa_codes%d" % z, [P, PACK, 2 * P], U8) for z in range(PASSES)]
+        wa_plane = [sbuf("wa_plane%d" % z, [P, PACK, P], U8) for z in range(PASSES)]
+        for z in range(PASSES):
+            nc.vector.tensor_copy(
+                out=wa_codes[z][:].bitcast(U16).rearrange("p t (c i) -> p c t i", i=8),
+                in_=wa_raw[:, z, :].bitcast(U16).rearrange("p (c i t) -> p c t i", i=8, t=PACK),
+            )
+            nc.vector.tensor_copy(
+                out=wa_plane[z][:].rearrange("p t (c i) -> p c t i", i=16),
+                in_=wa_raw_scales[:, z, :].rearrange("p (c i t) -> p c t i", i=16, t=PACK),
+            )
+
+        ga_bank = a_banks[BLOCKS - 1]
+        for c in range(PACK):
+            nc.tensor.transpose(ga_bank[:, c, :], ga_cols[:, c : c + 1].to_broadcast([P, P]), identity[:])
+        ga_rows = sbuf("ga_rows", [P, J], F32)
+        nc.scalar.copy(out=ga_rows[:].rearrange("p (n c) -> p n c", c=PACK), in_=ga_bank[:].rearrange("p c n -> p n c"))
+
+        def first_layer(z, b):
+            rhs, rhs_scale = x_operand(z, b)
+            for t in range(PACK):
+                nc.tensor.matmul_mx(
+                    out=a_banks[b][:, t, :],
+                    lhsT=wa_codes[z][:, t, :].bitcast(FP4X4),
+                    lhsT_scale=wa_plane[z][:, t, :],
+                    rhs=rhs,
+                    rhs_scale=rhs_scale,
+                    start=(z == 0 and t == 0),
+                    stop=(z == PASSES - 1 and t == PACK - 1),
+                )
+
+        def bypass(z, b):
+            rhs, rhs_scale = x_operand(z, b)
+            for i in range(N_TILES):
+                nc.tensor.matmul_mx(
+                    out=p_banks[b][:, i, :],
+                    lhsT=wc_codes[z][:, 2 * P * i : 2 * P * (i + 1)].bitcast(FP4X4),
+                    lhsT_scale=wc_plane[:, z, P * i : P * (i + 1)],
+                    rhs=rhs,
+                    rhs_scale=rhs_scale,
+                    start=(z == 0 and i == 0),
+                    stop=False,
+                )
+
+        for b in range(BLOCKS):
+            bypass(0, b)
+        for b in range(BLOCKS):
+            first_layer(0, b)
+
+        gather_words(1)
+        for b in range(BLOCKS):
+            first_layer(1, b)
+
+        hid = [sbuf("hid%d" % b, [P, BLOCK, PACK], BF16) for b in range(BLOCKS)]
+        hid_codes = [sbuf("hid_codes%d" % b, [P, BLOCK], U32) for b in range(BLOCKS)]
+        hid_plane = [sbuf("hid_plane%d" % b, [P, BLOCK], U8) for b in range(BLOCKS)]
+        result = [sbuf("result%d" % b, [P, N_TILES, BLOCK], F32) for b in range(BLOCKS)]
+        out_view = out.rearrange("(i p) j -> p i j", p=P)
+        for b in range(BLOCKS):
+            nc.scalar.activation(
+                out=hid[b][:], in_=a_banks[b][:].rearrange("p t j -> p j t"), func=mybir.ActivationFunctionType.Relu
+            )
+            nc.vector.quantize_mx(
+                out=hid_codes[b][:].bitcast(FP8X4), scales=hid_plane[b][:], in_=hid[b][:].rearrange("p j t -> p (j t)")
+            )
+        for b in range(BLOCKS):
+            bypass(1, b)
+            for i in range(N_TILES):
+                nc.tensor.matmul_mx(
+                    out=p_banks[b][:, i, :],
+                    lhsT=wb_codes[:, P * i : P * (i + 1)].bitcast(FP8X4),
+                    lhsT_scale=wb_plane[:, P * i : P * (i + 1)],
+                    rhs=hid_codes[b][:].bitcast(FP8X4),
+                    rhs_scale=hid_plane[b][:],
+                    start=False,
+                    stop=(i == N_TILES - 1),
+                )
+            tokens = slice(b * BLOCK, (b + 1) * BLOCK)
+            nc.vector.tensor_tensor(
+                out=result[b][:],
+                in0=p_banks[b][:],
+                in1=ga_rows[:, tokens].unsqueeze(1).to_broadcast([P, N_TILES, BLOCK]),
+                op=mybir.AluOpType.mult,
+            )
+            nc.sync.dma_start(out=out_view[:, :, tokens], in_=result[b][:])

@@ -23,6 +23,7 @@ BLOCK = 128
 BLOCKS = J // BLOCK
 HALF = 256
 N_TILES = N // P
+VECTOR_RELU_BLOCKS = (2,)
 
 
 def tile_list_expert_with_bypass_kernel(
@@ -41,69 +42,73 @@ def tile_list_expert_with_bypass_kernel(
         x_table_scales = sbuf("x_table_scales", [P, T], U8)
         wa_raw = sbuf("wa_raw", [P, PASSES, 2 * R], U8)
         wa_raw_scales = sbuf("wa_raw_scales", [P, PASSES, R], U8)
-        wc_codes = [sbuf("wc_codes%d" % z, [P, 2 * N], U8) for z in range(PASSES)]
+        wc_codes = [sbuf("wc_codes%d" % u, [P, PASSES, N], U8) for u in range(2)]
         wc_plane = sbuf("wc_plane", [P, PASSES, N], U8)
         wb_codes = sbuf("wb_codes", [P, N], I32)
-        wb_plane = sbuf("wb_plane", [P, N], U8)
-        x_plane1 = sbuf("x_plane1", [P, J], U8)
+        wb_plane = sbuf("wb_plane", [P, 1, N], U8)
+        x_planes = [sbuf("x_plane%d" % z, [P, J], U8) for z in range(PASSES)]
         ga_cols = sbuf("ga_cols", [P, PACK], F32)
         identity = sbuf("identity", [P, P], F32)
 
         a_banks = [psum.tile([P, PACK, BLOCK], F32, name="a_bank%d" % b) for b in range(BLOCKS)]
-        p_banks = [psum.tile([P, N_TILES, BLOCK], F32, name="p_bank%d" % b) for b in range(BLOCKS)]
+        p_banks = [psum.tile([P, J], F32, name="p_bank%d" % i) for i in range(N_TILES)]
 
-        for plane in (x_table_scales, wa_raw_scales, wc_plane, wb_plane, x_plane1):
+        for plane in (x_table_scales, wa_raw_scales, wc_plane, wb_plane, x_planes[1]):
             nc.vector.memset(plane[:].bitcast(I32), 0)
 
         def words(dram):
             return dram.rearrange("p c t -> p (c t)").bitcast(I32)
 
-        def load_plane(queue, plane, scales):
-            for q in range(QUADRANTS):
-                queue.dma_start(
-                    out=plane[32 * q : 32 * q + 4].bitcast(I32),
-                    in_=scales[:, 4 * q : 4 * q + 4, :].rearrange("z r c -> r z c").bitcast(I32),
-                )
+        def load_scale_rows(queue, plane, scales, q):
+            queue.dma_start(
+                out=plane[32 * q : 32 * q + 4].bitcast(I32),
+                in_=scales[:, 4 * q : 4 * q + 4, :].rearrange("z r c -> r z c").bitcast(I32),
+            )
 
-        nc.sync.dma_start(out=wa_raw[:].bitcast(I32), in_=wa_words.rearrange("z p c -> p z c").bitcast(I32))
-        for q in range(QUADRANTS):
-            nc.scalar.dma_start(
+        def load_x_scale_rows(queue, q):
+            queue.dma_start(
                 out=x_table_scales[32 * q : 32 * q + 8, :].bitcast(I32),
                 in_=xq_scales[:, 4 * q : 4 * q + 4, :].bitcast(I32),
             )
-        nc.sync.dma_start(offsets[:], offs)
-        nc.sync.dma_start(out=ga_cols[:], in_=ga[0].rearrange("(p c) -> p c", c=PACK))
-        nc.sync.dma_start(out=x_table[0][:], in_=words(xq_words[0]))
-        nc.sync.dma_start(out=wc_codes[0][:].bitcast(I32), in_=wc_words[0].bitcast(I32))
-        nc.sync.dma_start(out=x_table[1][:], in_=words(xq_words[1]))
-        load_plane(nc.scalar, wa_raw_scales, wa_scales)
-        make_identity(nc, identity[:])
-        load_plane(nc.gpsimd, wc_plane, wc_scales)
-        nc.sync.dma_start(out=wc_codes[1][:].bitcast(I32), in_=wc_words[1].bitcast(I32))
-        nc.sync.dma_start(out=wb_codes[:], in_=words(wb_words[0]))
 
-        x_plane0 = sbuf("x_plane0", [P, J], U8)
-        nc.vector.tensor_copy(out=x_plane0[:], in_=x_table_scales[:].indirect(offsets[:]))
-        nc.scalar.dma_start(out=x_plane1[0:100, :].bitcast(I32), in_=x_plane0[4:104, :].bitcast(I32))
-        x_planes = [x_plane0, x_plane1]
-        for q in range(QUADRANTS):
-            nc.scalar.dma_start(
-                out=wb_plane[32 * q : 32 * q + 4, :].bitcast(I32),
-                in_=wb_scales[0, 4 * q : 4 * q + 4, :].bitcast(I32),
+        def load_wc(u):
+            nc.sync.dma_start(
+                out=wc_codes[u][:].bitcast(I32),
+                in_=wc_words[:, :, N * u : N * (u + 1)].rearrange("z p c -> p z c").bitcast(I32),
             )
 
-        x_codes = [[sbuf("x_codes%d_%d" % (z, h), [P, HALF], U32) for h in range(J // HALF)] for z in range(PASSES)]
+        make_identity(nc, identity[:])
+        nc.sync.dma_start(out=wa_raw[:].bitcast(I32), in_=wa_words.rearrange("z p c -> p z c").bitcast(I32))
+        nc.sync.dma_start(offsets[:], offs)
+        nc.scalar.dma_start(out=ga_cols[:], in_=ga[0].rearrange("(p c) -> p c", c=PACK))
+        for q in range(QUADRANTS):
+            load_x_scale_rows(nc.sync if q < 2 else nc.scalar, q)
+        nc.sync.dma_start(out=x_table[0][:], in_=words(xq_words[0]))
+        for q in range(QUADRANTS):
+            load_scale_rows(nc.sync, wa_raw_scales, wa_scales, q)
+        nc.sync.dma_start(out=x_table[1][:], in_=words(xq_words[1]))
+        for q in range(2):
+            load_scale_rows(nc.sync, wc_plane, wc_scales, q)
+
+        nc.vector.tensor_copy(out=x_planes[0][:], in_=x_table_scales[:].indirect(offsets[:]))
+        nc.sync.dma_start(out=x_planes[1][0:112, :].bitcast(I32), in_=x_planes[0][4:116, :].bitcast(I32))
+        load_wc(0)
+        for q in range(2, QUADRANTS):
+            load_scale_rows(nc.sync, wc_plane, wc_scales, q)
+        nc.sync.dma_start(out=wb_codes[:], in_=words(wb_words[0]))
+        for q in range(QUADRANTS):
+            load_scale_rows(nc.sync, wb_plane, wb_scales, q)
+        load_wc(1)
+
+        x_codes = [sbuf("x_codes%d" % z, [P, J], U32) for z in range(PASSES)]
 
         def gather_words(z):
             for h in range(J // HALF):
                 cols = slice(h * HALF // 16, (h + 1) * HALF // 16)
-                nc.vector.tensor_copy(out=x_codes[z][h][:], in_=x_table[z][:].bitcast(U32).indirect(offsets[:, cols]))
-
-        def x_operand(z, b):
-            h, i = divmod(b * BLOCK, HALF)
-            return x_codes[z][h][:, i : i + BLOCK].bitcast(FP8X4), x_planes[z][:, b * BLOCK : (b + 1) * BLOCK]
-
-        gather_words(0)
+                nc.vector.tensor_copy(
+                    out=x_codes[z][:, h * HALF : (h + 1) * HALF],
+                    in_=x_table[z][:].bitcast(U32).indirect(offsets[:, cols]),
+                )
 
         wa_codes = [sbuf("wa_codes%d" % z, [P, PACK, 2 * P], U8) for z in range(PASSES)]
         wa_plane = [sbuf("wa_plane%d" % z, [P, PACK, P], U8) for z in range(PASSES)]
@@ -112,81 +117,110 @@ def tile_list_expert_with_bypass_kernel(
                 out=wa_codes[z][:].bitcast(U16).rearrange("p t (c i) -> p c t i", i=8),
                 in_=wa_raw[:, z, :].bitcast(U16).rearrange("p (c i t) -> p c t i", i=8, t=PACK),
             )
+        for z in range(PASSES):
             nc.vector.tensor_copy(
                 out=wa_plane[z][:].rearrange("p t (c i) -> p c t i", i=16),
                 in_=wa_raw_scales[:, z, :].rearrange("p (c i t) -> p c t i", i=16, t=PACK),
             )
+        gather_words(0)
 
-        ga_bank = a_banks[BLOCKS - 1]
+        ga_rows = sbuf("ga_rows", [P, P, PACK], F32)
         for c in range(PACK):
-            nc.tensor.transpose(ga_bank[:, c, :], ga_cols[:, c : c + 1].to_broadcast([P, P]), identity[:])
-        ga_rows = sbuf("ga_rows", [P, J], F32)
-        nc.scalar.copy(out=ga_rows[:].rearrange("p (n c) -> p n c", c=PACK), in_=ga_bank[:].rearrange("p c n -> p n c"))
+            nc.tensor.transpose(a_banks[c][:, 0, :], ga_cols[:, c : c + 1].to_broadcast([P, P]), identity[:])
+            nc.scalar.copy(out=ga_rows[:, :, c], in_=a_banks[c][:, 0, :])
+        ga_flat = ga_rows[:].rearrange("p n c -> p (n c)")
+
+        for b in range(3):
+            nc.tensor.matmul_mx(
+                out=a_banks[b][:].rearrange("p t j -> p (t j)"),
+                lhsT=x_table[0][:, 0:P].bitcast(FP8X4),
+                lhsT_scale=x_table_scales[:, 0:P],
+                rhs=x_table[0][:, 0:J].bitcast(FP8X4),
+                rhs_scale=x_table_scales[:, 0:J],
+                start=True,
+                stop=True,
+            )
 
         def first_layer(z, b):
-            rhs, rhs_scale = x_operand(z, b)
+            tokens = slice(b * BLOCK, (b + 1) * BLOCK)
             for t in range(PACK):
                 nc.tensor.matmul_mx(
                     out=a_banks[b][:, t, :],
                     lhsT=wa_codes[z][:, t, :].bitcast(FP4X4),
                     lhsT_scale=wa_plane[z][:, t, :],
-                    rhs=rhs,
-                    rhs_scale=rhs_scale,
+                    rhs=x_codes[z][:, tokens].bitcast(FP8X4),
+                    rhs_scale=x_planes[z][:, tokens],
                     start=(z == 0 and t == 0),
                     stop=(z == PASSES - 1 and t == PACK - 1),
                 )
 
-        def bypass(z, b):
-            rhs, rhs_scale = x_operand(z, b)
-            for i in range(N_TILES):
-                nc.tensor.matmul_mx(
-                    out=p_banks[b][:, i, :],
-                    lhsT=wc_codes[z][:, 2 * P * i : 2 * P * (i + 1)].bitcast(FP4X4),
-                    lhsT_scale=wc_plane[:, z, P * i : P * (i + 1)],
-                    rhs=rhs,
-                    rhs_scale=rhs_scale,
-                    start=(z == 0 and i == 0),
-                    stop=False,
-                )
-
-        for b in range(BLOCKS):
-            bypass(0, b)
         for b in range(BLOCKS):
             first_layer(0, b)
-
         gather_words(1)
         for b in range(BLOCKS):
             first_layer(1, b)
 
         hid = [sbuf("hid%d" % b, [P, BLOCK, PACK], BF16) for b in range(BLOCKS)]
-        hid_codes = [sbuf("hid_codes%d" % b, [P, BLOCK], U32) for b in range(BLOCKS)]
-        hid_plane = [sbuf("hid_plane%d" % b, [P, BLOCK], U8) for b in range(BLOCKS)]
-        result = [sbuf("result%d" % b, [P, N_TILES, BLOCK], F32) for b in range(BLOCKS)]
-        out_view = out.rearrange("(i p) j -> p i j", p=P)
+        hid_codes = sbuf("hid_codes", [P, J], U32)
+        hid_plane = sbuf("hid_plane", [P, J], U8)
         for b in range(BLOCKS):
-            nc.scalar.activation(
-                out=hid[b][:], in_=a_banks[b][:].rearrange("p t j -> p j t"), func=mybir.ActivationFunctionType.Relu
-            )
-            nc.vector.quantize_mx(
-                out=hid_codes[b][:].bitcast(FP8X4), scales=hid_plane[b][:], in_=hid[b][:].rearrange("p j t -> p (j t)")
-            )
+            sums = a_banks[b][:].rearrange("p t j -> p j t")
+            if b in VECTOR_RELU_BLOCKS:
+                nc.vector.tensor_scalar_max(hid[b][:], sums, 0.0)
+            else:
+                nc.scalar.activation(out=hid[b][:], in_=sums, func=mybir.ActivationFunctionType.Relu)
         for b in range(BLOCKS):
-            bypass(1, b)
-            for i in range(N_TILES):
-                nc.tensor.matmul_mx(
-                    out=p_banks[b][:, i, :],
-                    lhsT=wb_codes[:, P * i : P * (i + 1)].bitcast(FP8X4),
-                    lhsT_scale=wb_plane[:, P * i : P * (i + 1)],
-                    rhs=hid_codes[b][:].bitcast(FP8X4),
-                    rhs_scale=hid_plane[b][:],
-                    start=False,
-                    stop=(i == N_TILES - 1),
-                )
             tokens = slice(b * BLOCK, (b + 1) * BLOCK)
-            nc.vector.tensor_tensor(
-                out=result[b][:],
-                in0=p_banks[b][:],
-                in1=ga_rows[:, tokens].unsqueeze(1).to_broadcast([P, N_TILES, BLOCK]),
-                op=mybir.AluOpType.mult,
+            nc.vector.quantize_mx(
+                out=hid_codes[:, tokens].bitcast(FP8X4),
+                scales=hid_plane[:, tokens],
+                in_=hid[b][:].rearrange("p j t -> p (j t)"),
             )
-            nc.sync.dma_start(out=out_view[:, :, tokens], in_=result[b][:])
+
+        def bypass(i):
+            u, v = divmod(i, 2)
+            for z in range(PASSES):
+                nc.tensor.matmul_mx(
+                    out=p_banks[i][:],
+                    lhsT=wc_codes[u][:, z, 2 * P * v : 2 * P * (v + 1)].bitcast(FP4X4),
+                    lhsT_scale=wc_plane[:, z, P * i : P * (i + 1)],
+                    rhs=x_codes[z][:].bitcast(FP8X4),
+                    rhs_scale=x_planes[z][:],
+                    start=(z == 0),
+                    stop=False,
+                )
+
+        def second_layer(i, tokens):
+            nc.tensor.matmul_mx(
+                out=p_banks[i][:, tokens],
+                lhsT=wb_codes[:, P * i : P * (i + 1)].bitcast(FP8X4),
+                lhsT_scale=wb_plane[:, 0, P * i : P * (i + 1)],
+                rhs=hid_codes[:, tokens].bitcast(FP8X4),
+                rhs_scale=hid_plane[:, tokens],
+                start=False,
+                stop=(tokens.stop == J),
+            )
+
+        def finish(i, tokens):
+            result = sbuf("result%d_%d" % (i, tokens.start), [P, tokens.stop - tokens.start], F32)
+            nc.vector.tensor_tensor(
+                out=result[:], in0=p_banks[i][:, tokens], in1=ga_flat[:, tokens], op=mybir.AluOpType.mult
+            )
+            nc.sync.dma_start(out=out[P * i : P * (i + 1), tokens], in_=result[:])
+
+        halves = [slice(0, HALF), slice(HALF, J)]
+        every = slice(0, J)
+        bypass(0)
+        bypass(1)
+        for tokens in halves:
+            second_layer(0, tokens)
+            second_layer(1, tokens)
+        finish(0, every)
+        finish(1, every)
+        bypass(2)
+        second_layer(2, every)
+        finish(2, every)
+        bypass(3)
+        second_layer(3, every)
+        for tokens in halves:
+            finish(3, tokens)

@@ -61,14 +61,14 @@ def tile_list_expert_with_bypass_kernel(
 
         def load_scale_rows(queue, plane, scales, q):
             queue.dma_start(
-                out=plane[32 * q : 32 * q + 4].bitcast(I32),
-                in_=scales[:, 4 * q : 4 * q + 4, :].rearrange("z r c -> r z c").bitcast(I32),
+                out=plane[q:P:32].bitcast(I32),
+                in_=scales[:, q:16:4, :].rearrange("z r c -> r z c").bitcast(I32),
             )
 
         def load_x_scale_rows(queue, q):
             queue.dma_start(
-                out=x_table_scales[32 * q : 32 * q + 8, :].bitcast(I32),
-                in_=xq_scales[:, 4 * q : 4 * q + 4, :].bitcast(I32),
+                out=x_table_scales[q:P:16, :].bitcast(I32),
+                in_=xq_scales[:, q:16:4, :].rearrange("z r c -> r z c").bitcast(I32),
             )
 
         def load_wc(u):
@@ -77,7 +77,8 @@ def tile_list_expert_with_bypass_kernel(
                 in_=wc_words[:, :, N * u : N * (u + 1)].rearrange("z p c -> p z c").bitcast(I32),
             )
 
-        make_identity(nc, identity[:])
+        nc.vector.memset(identity[:], 0.0)
+        make_identity(nc, identity[:], nomemset=True)
         nc.sync.dma_start(out=wa_raw[:].bitcast(I32), in_=wa_words.rearrange("z p c -> p z c").bitcast(I32))
         nc.sync.dma_start(offsets[:], offs)
         nc.scalar.dma_start(out=ga_cols[:], in_=ga[0].rearrange("(p c) -> p c", c=PACK))
@@ -87,11 +88,11 @@ def tile_list_expert_with_bypass_kernel(
         for q in range(QUADRANTS):
             load_scale_rows(nc.sync, wa_raw_scales, wa_scales, q)
         nc.sync.dma_start(out=x_table[1][:], in_=words(xq_words[1]))
-        for q in range(2):
-            load_scale_rows(nc.sync, wc_plane, wc_scales, q)
 
         nc.vector.tensor_copy(out=x_planes[0][:], in_=x_table_scales[:].indirect(offsets[:]))
-        nc.sync.dma_start(out=x_planes[1][0:112, :].bitcast(I32), in_=x_planes[0][4:116, :].bitcast(I32))
+        nc.sync.dma_start(out=x_planes[1][0:112, :].bitcast(I32), in_=x_planes[0][16:128, :].bitcast(I32))
+        for q in range(2):
+            load_scale_rows(nc.sync, wc_plane, wc_scales, q)
         load_wc(0)
         for q in range(2, QUADRANTS):
             load_scale_rows(nc.sync, wc_plane, wc_scales, q)

from contextlib import ExitStack

import concourse.mybir as mybir
from concourse.masks import make_identity

K, T, J, N, R = 1024, 2048, 512, 512, 512
FLOPS = 2 * J * (K * R + R * N + K * N)

F32 = mybir.dt.float32
BF16 = mybir.dt.bfloat16
I32 = mybir.dt.int32
U32 = mybir.dt.uint32
U16 = mybir.dt.uint16
U8 = mybir.dt.uint8
FP8X4 = mybir.dt.float8_e4m3fn_x4
FP4X4 = mybir.dt.float4_e2m1fn_x4

P = 128
PACK = 4
PASSES = K // (P * PACK)
QUADRANTS = 4
BLOCK = 128
BLOCKS = J // BLOCK
HALF = 256
N_TILES = N // P
VECTOR_RELU_BLOCKS = (2,)


def tile_list_expert_with_bypass_kernel(
    tc, xq_words, xq_scales, wa_words, wa_scales, wb_words, wb_scales, wc_words, wc_scales, ga, offs, out
):
    nc = tc.nc
    with ExitStack() as ctx:
        keep = ctx.enter_context(tc.tile_pool(name="keep", bufs=1))
        psum = ctx.enter_context(tc.psum_pool(name="psum", bufs=1))

        def sbuf(name, shape, dtype):
            return keep.tile(shape, dtype, name=name, align_bytes=64)

        offsets = keep.tile([P, J // 16], U16, name="offsets")
        x_table = [sbuf("x_table%d" % z, [P, T], I32) for z in range(PASSES)]
        x_table_scales = sbuf("x_table_scales", [P, T], U8)
        wa_raw = sbuf("wa_raw", [P, PASSES, 2 * R], U8)
        wa_raw_scales = sbuf("wa_raw_scales", [P, PASSES, R], U8)
        wc_codes = [sbuf("wc_codes%d" % u, [P, PASSES, N], U8) for u in range(2)]
        wc_plane = sbuf("wc_plane", [P, PASSES, N], U8)
        wb_codes = sbuf("wb_codes", [P, N], I32)
        wb_plane = sbuf("wb_plane", [P, 1, N], U8)
        x_planes = [sbuf("x_plane%d" % z, [P, J], U8) for z in range(PASSES)]
        ga_cols = sbuf("ga_cols", [P, PACK], F32)
        identity = sbuf("identity", [P, P], F32)

        a_banks = [psum.tile([P, PACK, BLOCK], F32, name="a_bank%d" % b) for b in range(BLOCKS)]
        p_banks = [psum.tile([P, J], F32, name="p_bank%d" % i) for i in range(N_TILES)]

        for plane in (x_table_scales, wa_raw_scales, wc_plane, wb_plane, x_planes[1]):
            nc.vector.memset(plane[:].bitcast(I32), 0)

        def words(dram):
            return dram.rearrange("p c t -> p (c t)").bitcast(I32)

        def load_scale_rows(queue, plane, scales, q):
            queue.dma_start(
                out=plane[q:P:32].bitcast(I32),
                in_=scales[:, q:16:4, :].rearrange("z r c -> r z c").bitcast(I32),
            )

        def load_x_scale_rows(queue, q):
            queue.dma_start(
                out=x_table_scales[q:P:16, :].bitcast(I32),
                in_=xq_scales[:, q:16:4, :].rearrange("z r c -> r z c").bitcast(I32),
            )

        def load_wc(u):
            nc.sync.dma_start(
                out=wc_codes[u][:].bitcast(I32),
                in_=wc_words[:, :, N * u : N * (u + 1)].rearrange("z p c -> p z c").bitcast(I32),
            )

        nc.vector.memset(identity[:], 0.0)
        make_identity(nc, identity[:], nomemset=True)
        nc.sync.dma_start(out=wa_raw[:].bitcast(I32), in_=wa_words.rearrange("z p c -> p z c").bitcast(I32))
        nc.sync.dma_start(offsets[:], offs)
        nc.scalar.dma_start(out=ga_cols[:], in_=ga[0].rearrange("(p c) -> p c", c=PACK))
        for q in range(QUADRANTS):
            load_x_scale_rows(nc.sync if q < 2 else nc.scalar, q)
        nc.sync.dma_start(out=x_table[0][:], in_=words(xq_words[0]))
        for q in range(QUADRANTS):
            load_scale_rows(nc.sync, wa_raw_scales, wa_scales, q)
        nc.sync.dma_start(out=x_table[1][:], in_=words(xq_words[1]))

        nc.vector.tensor_copy(out=x_planes[0][:], in_=x_table_scales[:].indirect(offsets[:]))
        nc.sync.dma_start(out=x_planes[1][0:112, :].bitcast(I32), in_=x_planes[0][16:128, :].bitcast(I32))
        for q in range(2):
            load_scale_rows(nc.sync, wc_plane, wc_scales, q)
        load_wc(0)
        for q in range(2, QUADRANTS):
            load_scale_rows(nc.sync, wc_plane, wc_scales, q)
        nc.sync.dma_start(out=wb_codes[:], in_=words(wb_words[0]))
        for q in range(QUADRANTS):
            load_scale_rows(nc.sync, wb_plane, wb_scales, q)
        load_wc(1)

        x_codes = [sbuf("x_codes%d" % z, [P, J], U32) for z in range(PASSES)]

        def gather_words(z):
            for h in range(J // HALF):
                cols = slice(h * HALF // 16, (h + 1) * HALF // 16)
                nc.vector.tensor_copy(
                    out=x_codes[z][:, h * HALF : (h + 1) * HALF],
                    in_=x_table[z][:].bitcast(U32).indirect(offsets[:, cols]),
                )

        wa_codes = [sbuf("wa_codes%d" % z, [P, PACK, 2 * P], U8) for z in range(PASSES)]
        wa_plane = [sbuf("wa_plane%d" % z, [P, PACK, P], U8) for z in range(PASSES)]
        for z in range(PASSES):
            nc.vector.tensor_copy(
                out=wa_codes[z][:].bitcast(U16).rearrange("p t (c i) -> p c t i", i=8),
                in_=wa_raw[:, z, :].bitcast(U16).rearrange("p (c i t) -> p c t i", i=8, t=PACK),
            )
        for z in range(PASSES):
            nc.vector.tensor_copy(
                out=wa_plane[z][:].rearrange("p t (c i) -> p c t i", i=16),
                in_=wa_raw_scales[:, z, :].rearrange("p (c i t) -> p c t i", i=16, t=PACK),
            )
        gather_words(0)

        ga_rows = sbuf("ga_rows", [P, P, PACK], F32)
        for c in range(PACK):
            nc.tensor.transpose(a_banks[c][:, 0, :], ga_cols[:, c : c + 1].to_broadcast([P, P]), identity[:])
            nc.scalar.copy(out=ga_rows[:, :, c], in_=a_banks[c][:, 0, :])
        ga_flat = ga_rows[:].rearrange("p n c -> p (n c)")

        for b in range(3):
            nc.tensor.matmul_mx(
                out=a_banks[b][:].rearrange("p t j -> p (t j)"),
                lhsT=x_table[0][:, 0:P].bitcast(FP8X4),
                lhsT_scale=x_table_scales[:, 0:P],
                rhs=x_table[0][:, 0:J].bitcast(FP8X4),
                rhs_scale=x_table_scales[:, 0:J],
                start=True,
                stop=True,
            )

        def first_layer(z, b):
            tokens = slice(b * BLOCK, (b + 1) * BLOCK)
            for t in range(PACK):
                nc.tensor.matmul_mx(
                    out=a_banks[b][:, t, :],
                    lhsT=wa_codes[z][:, t, :].bitcast(FP4X4),
                    lhsT_scale=wa_plane[z][:, t, :],
                    rhs=x_codes[z][:, tokens].bitcast(FP8X4),
                    rhs_scale=x_planes[z][:, tokens],
                    start=(z == 0 and t == 0),
                    stop=(z == PASSES - 1 and t == PACK - 1),
                )

        for b in range(BLOCKS):
            first_layer(0, b)
        gather_words(1)
        for b in range(BLOCKS):
            first_layer(1, b)

        hid = [sbuf("hid%d" % b, [P, BLOCK, PACK], BF16) for b in range(BLOCKS)]
        hid_codes = sbuf("hid_codes", [P, J], U32)
        hid_plane = sbuf("hid_plane", [P, J], U8)
        for b in range(BLOCKS):
            sums = a_banks[b][:].rearrange("p t j -> p j t")
            if b in VECTOR_RELU_BLOCKS:
                nc.vector.tensor_scalar_max(hid[b][:], sums, 0.0)
            else:
                nc.scalar.activation(out=hid[b][:], in_=sums, func=mybir.ActivationFunctionType.Relu)
        for b in range(BLOCKS):
            tokens = slice(b * BLOCK, (b + 1) * BLOCK)
            nc.vector.quantize_mx(
                out=hid_codes[:, tokens].bitcast(FP8X4),
                scales=hid_plane[:, tokens],
                in_=hid[b][:].rearrange("p j t -> p (j t)"),
            )

        def bypass(i):
            u, v = divmod(i, 2)
            for z in range(PASSES):
                nc.tensor.matmul_mx(
                    out=p_banks[i][:],
                    lhsT=wc_codes[u][:, z, 2 * P * v : 2 * P * (v + 1)].bitcast(FP4X4),
                    lhsT_scale=wc_plane[:, z, P * i : P * (i + 1)],
                    rhs=x_codes[z][:].bitcast(FP8X4),
                    rhs_scale=x_planes[z][:],
                    start=(z == 0),
                    stop=False,
                )

        def second_layer(i, tokens):
            nc.tensor.matmul_mx(
                out=p_banks[i][:, tokens],
                lhsT=wb_codes[:, P * i : P * (i + 1)].bitcast(FP8X4),
                lhsT_scale=wb_plane[:, 0, P * i : P * (i + 1)],
                rhs=hid_codes[:, tokens].bitcast(FP8X4),
                rhs_scale=hid_plane[:, tokens],
                start=False,
                stop=(tokens.stop == J),
            )

        def finish(i, tokens):
            result = sbuf("result%d_%d" % (i, tokens.start), [P, tokens.stop - tokens.start], F32)
            nc.vector.tensor_tensor(
                out=result[:], in0=p_banks[i][:, tokens], in1=ga_flat[:, tokens], op=mybir.AluOpType.mult
            )
            nc.sync.dma_start(out=out[P * i : P * (i + 1), tokens], in_=result[:])

        halves = [slice(0, HALF), slice(HALF, J)]
        every = slice(0, J)
        bypass(0)
        bypass(1)
        for tokens in halves:
            second_layer(0, tokens)
            second_layer(1, tokens)
        finish(0, every)
        finish(1, every)
        bypass(2)
        second_layer(2, every)
        finish(2, every)
        bypass(3)
        second_layer(3, every)
        for tokens in halves:
            finish(3, tokens)
